import numpy as np
import ml_dtypes


def mxq(x, axis, fmt="e4m3"):
    dtype, down = {"e4m3": (ml_dtypes.float8_e4m3fn, 7), "e5m2": (ml_dtypes.float8_e5m2, 14)}[fmt]
    v = np.moveaxis(np.asarray(x, np.float32).astype(ml_dtypes.bfloat16).astype(np.float64), axis, -1)
    blocks = v.reshape(v.shape[:-1] + (-1, 32))
    amax = np.abs(blocks).max(-1, keepdims=True)
    byte = np.maximum(np.where(amax > 0, np.frexp(amax)[1] - 1 + 127, 0) - down, 1)
    scale = np.exp2(byte - 127.0)
    codes = (blocks / scale).astype(np.float32).astype(dtype).astype(np.float64)
    return np.moveaxis((codes * scale).reshape(v.shape), -1, axis)


WIDE = False


def mx_kscale(k):
    if not WIDE:
        return np.ones(k)
    levels = np.array([10, -10, 5, -5, 0])
    if k % 512:
        return np.exp2(np.random.permutation(np.resize(levels, k // 32))).repeat(32)
    a = np.empty((k // 512, 16))
    for p in range(k // 512):
        a[p, :8] = np.random.permutation(np.resize(levels, 8))
        for g in range(8):
            far = levels[np.abs(levels - a[p, g]) >= 10]
            a[p, g + 8] = far[np.random.randint(len(far))]
    return np.exp2(a.ravel()).repeat(32)


BF16 = ml_dtypes.bfloat16


def bf(x):
    return np.asarray(x, np.float32).astype(BF16)


def f64(x):
    return np.asarray(x).astype(np.float64)


C, K, D, B, L = 1536, 1024, 1024, 1024, 512


def draw0():
    s, u, v = mx_kscale(K), mx_kscale(C), mx_kscale(L)
    phi = np.random.standard_normal((C, K)) * s
    w = np.random.standard_normal((K, D)) / np.sqrt(K) / s[:, None]
    j_nom = 0.5 * np.random.standard_normal((C, D))
    act = np.random.uniform(0.3, 1.0, C) * u
    force = np.abs(np.random.standard_normal((B, C))) / np.sqrt(C) / u
    pose = np.random.standard_normal((B, L)) * v
    wg = np.random.standard_normal((L, D)) / np.sqrt(L) / v[:, None]
    return {"phi": bf(phi), "w": bf(w), "j_nom": bf(j_nom), "act": bf(act),
            "force": bf(force), "pose": bf(pose), "wg": bf(wg)}


def core(phi, w, j_nom, act, force, pose, wg):
    corr = mxq(f64(phi), 1, "e4m3") @ mxq(f64(w), 0, "e4m3")
    jac = (corr + f64(j_nom)) * f64(act)[:, None]
    contact = mxq(f64(force), 1, "e4m3") @ mxq(jac, 0, "e4m3")
    grav = mxq(f64(pose), 1, "e4m3") @ mxq(f64(wg), 0, "e4m3")
    return contact + grav


def e4m3fn_bytes(y):
    return np.clip(np.asarray(y, np.float64), -448.0, 448.0).astype(np.float32).astype(ml_dtypes.float8_e4m3fn).view(np.uint8)


def e4m3fn_values(b):
    return np.asarray(b, np.uint8).view(ml_dtypes.float8_e4m3fn).astype(np.float64)


def setup_inputs():
    d = draw0()
    x0 = np.asarray(d['phi']).astype(np.float64)
    s = (np.max(np.abs(x0), axis=(0,), keepdims=True) / 448.0).astype(np.float32)
    out = {}
    for k, v in d.items():
        if k == 'phi':
            out['phi_bytes'] = e4m3fn_bytes(x0 / s.astype(np.float64))
            out['phi_scale'] = s
        else:
            out[k] = v
    return out


def reference(phi_bytes, phi_scale, w, j_nom, act, force, pose, wg):
    return core(e4m3fn_values(phi_bytes) * phi_scale.astype(np.float64), w, j_nom, act, force, pose, wg)

@@ -1,0 +1,462 @@
+from contextlib import ExitStack
+
+import concourse.mybir as mybir
+from concourse.masks import make_identity
+
+C, K, D, B, L = 1536, 1024, 1024, 1024, 512
+FLOPS = 2 * C * K * D + 2 * B * C * D + 2 * B * L * D
+
+F32 = mybir.dt.float32
+BF16 = mybir.dt.bfloat16
+U32 = mybir.dt.uint32
+U8 = mybir.dt.uint8
+FP8 = mybir.dt.float8_e4m3fn
+FP8X4 = mybir.dt.float8_e4m3fn_x4
+MULT = mybir.AluOpType.mult
+ADD = mybir.AluOpType.add
+COPY = mybir.ActivationFunctionType.Copy
+
+
+def tile_contact_jacobian_torque_s7_kernel(tc, phi_bytes, phi_scale, w, j_nom, act, force, pose, wg, out):
+    nc = tc.nc
+    V = nc.vector
+    S = nc.scalar
+    with ExitStack() as ctx:
+        keep = ctx.enter_context(tc.tile_pool(name="keep", bufs=1))
+        work = ctx.enter_context(tc.tile_pool(name="work", bufs=1))
+        psum = ctx.enter_context(tc.psum_pool(name="psum", bufs=8))
+        ctx.enter_context(tc.manual_schedule())
+
+        ident = keep.tile([128, 128], F32, name="ident")
+        make_identity(nc, ident[:])
+
+        scale = keep.tile([128, K], F32, name="scale")
+        nc.scalar.dma_start(out=scale[:], in_=phi_scale.rearrange("o k -> (o k)").partition_broadcast(128))
+        act16 = keep.tile([128, 3, 4], BF16, name="act16")
+        nc.scalar.dma_start(out=act16[:], in_=act.rearrange("(g p t) -> p g t", p=128, t=4))
+        act32 = keep.tile([128, 3, 4], F32, name="act32")
+
+        held = {}
+        w_v = w.rearrange("(g p t) n -> g p t n", p=128, t=4)
+        phi_v = phi_bytes.rearrange("(g m t) k -> g m t k", m=128, t=4)
+        jn_v = j_nom.rearrange("(g m t) d -> g m t d", m=128, t=4)
+        force_v = force.rearrange("(p j) c -> p j c", j=8)
+        pose_v = pose.rearrange("(p j) l -> p j l", j=8)
+        wg_v = wg.rearrange("(p t) n -> p t n", t=4)
+        out_v = out.rearrange("(p j) d -> j p d", j=8)
+
+        raw = {}
+
+        def raw_tile(key):
+            t = work.tile([128, 4, 512], BF16, name="raw", tag="raw", bufs=5, align_bytes=64)
+            raw[key] = t
+            return t
+
+        phi_raw = {}
+        jn_raw = [work.tile([128, 4, D], BF16, name="jn_raw%d" % g, tag="jn_raw", bufs=3, align_bytes=64) for g in range(3)]
+        f_raw = [work.tile([128, 2, C], BF16, name="f_raw%d" % i, tag="f_raw", bufs=4, align_bytes=64) for i in range(4)]
+
+        def ld_w(g, h):
+            x = raw_tile(("w", g, h))
+            nc.sync.dma_start(out=x[:], in_=w_v[g][:, :, 512 * h:512 * (h + 1)])
+
+        def ld_phi(G):
+            phi_raw[G] = work.tile([128, 4, K], U8, name="phi_raw", tag="phi_raw", bufs=3, align_bytes=64)
+            nc.sync.dma_start(out=phi_raw[G][:], in_=phi_v[G])
+
+        def ld_jn(G):
+            nc.sync.dma_start(out=jn_raw[G][:], in_=jn_v[G])
+
+        def ld_force(i):
+            nc.sync.dma_start(out=f_raw[i][:], in_=force_v[:, 2 * i:2 * i + 2, :])
+
+        def ld_wg(h):
+            x = raw_tile(("wg", h))
+            nc.sync.dma_start(out=x[:], in_=wg_v[:, :, 512 * h:512 * (h + 1)])
+
+        def ld_pose(jh):
+            x = raw_tile(("p", jh))
+            nc.sync.dma_start(out=x[:], in_=pose_v[:, 4 * jh:4 * jh + 4, :])
+
+        def cast_act():
+            nc.vector.tensor_copy(out=act32[:], in_=act16[:])
+
+
+        phi_c = keep.tile([128, 3, 2, 512], U32, name="phi_c", align_bytes=64)
+        phi_s = keep.tile([128, 3, 2, 512], U8, name="phi_s", align_bytes=64)
+        w_c = keep.tile([128, 2, D], U32, name="w_c", align_bytes=64)
+        w_s = keep.tile([128, 2, D], U8, name="w_s", align_bytes=64)
+        jac_c = keep.tile([128, 3, D], U32, name="jac_c", align_bytes=64)
+        jac_s = keep.tile([128, 3, D], U8, name="jac_s", align_bytes=64)
+        f_c = keep.tile([128, 3, B], U32, name="f_c", align_bytes=64)
+        f_s = keep.tile([128, 3, B], U8, name="f_s", align_bytes=64)
+        p_c = keep.tile([128, B], U32, name="p_c", align_bytes=64)
+        p_s = keep.tile([128, B], U8, name="p_s", align_bytes=64)
+        wg_c = keep.tile([128, D], U32, name="wg_c", align_bytes=64)
+        wg_s = keep.tile([128, D], U8, name="wg_s", align_bytes=64)
+
+        def grp_tile(key):
+            t = work.tile([128, 512, 4], BF16, name="grp", tag="grp", bufs=6, align_bytes=64)
+            held[key] = t
+            return t
+
+        def bank(key):
+            t = psum.tile([128, 512], F32, name="bank", tag="bank", bufs=8)
+            held[key] = t
+            return t
+
+        def copy_on(eng, dst, src):
+            if eng is V:
+                nc.vector.tensor_copy(out=dst, in_=src)
+            else:
+                nc.scalar.copy(out=dst, in_=src)
+
+        def interleave(eng, key, src):
+            t = grp_tile(key)
+            copy_on(eng, t[:].rearrange("p (c i) t -> p c t i", i=4), src.rearrange("p t (c i) -> p c t i", i=4))
+
+        def quantize(key, codes, scales):
+            nc.vector.quantize_mx(out=codes.bitcast(FP8X4), scales=scales, in_=held[key][:].rearrange("p n t -> p (n t)"))
+
+        def il_w(g, h, eng):
+            interleave(eng, ("w", g, h), raw["w", g, h][:])
+
+        def q_w(g, h):
+            cols = slice(512 * h, 512 * (h + 1))
+            quantize(("w", g, h), w_c[:, g, cols], w_s[:, g, cols])
+
+        def il_wg(h, eng):
+            interleave(eng, ("wg", h), raw["wg", h][:])
+
+        def q_wg(h):
+            cols = slice(512 * h, 512 * (h + 1))
+            quantize(("wg", h), wg_c[:, cols], wg_s[:, cols])
+
+        def prod(G, t):
+            x = work.tile([128, K], BF16, name="ph", tag="ph", bufs=4, align_bytes=64)
+            held["ph", G, t] = x
+            nc.vector.tensor_tensor(out=x[:], in0=phi_raw[G][:, t, :].bitcast(FP8), in1=scale[:], op=MULT)
+
+        def flip_phi(G, t):
+            words = held["ph", G, t][:].bitcast(F32)
+            x = bank(("flip", G, t))
+            x4 = x[:].rearrange("p (g u m) -> p g u m", g=2, u=2)
+            for g in range(2):
+                for u in range(2):
+                    nc.tensor.transpose(x4[:, g, u, :], words[:, 256 * g + u:256 * (g + 1):2], ident[:])
+
+        def exit_phi(G, t):
+            if ("gphi", G) not in held:
+                held["gphi", G] = work.tile([128, 2, 512, 4], BF16, name="gphi", tag="gphi", bufs=2, align_bytes=64)
+            x4 = held["flip", G, t][:].rearrange("p (g u m) -> p g u m", g=2, u=2)
+            dst = held["gphi", G][:].rearrange("p g n t -> p (g n t)").bitcast(F32).rearrange("p (g n u) -> p g n u", g=2, u=2)
+            nc.scalar.copy(out=dst[:, :, 128 * t:128 * (t + 1), :], in_=x4.rearrange("p g u m -> p g m u"))
+
+        def q_phi(G):
+            nc.vector.quantize_mx(
+                out=phi_c[:, G, :, :].rearrange("p g n -> p (g n)").bitcast(FP8X4),
+                scales=phi_s[:, G, :, :].rearrange("p g n -> p (g n)"),
+                in_=held["gphi", G][:].rearrange("p g n t -> p (g n t)"),
+            )
+
+        def mm1(G, h):
+            cols = slice(512 * h, 512 * (h + 1))
+            for t in range(4):
+                x = bank(("corr", G, h, t))
+                for g in range(2):
+                    nc.tensor.matmul_mx(
+                        out=x[:],
+                        lhsT=phi_c[:, G, g, 128 * t:128 * (t + 1)].bitcast(FP8X4),
+                        lhsT_scale=phi_s[:, G, g, 128 * t:128 * (t + 1)],
+                        rhs=w_c[:, g, cols].bitcast(FP8X4),
+                        rhs_scale=w_s[:, g, cols],
+                        start=(g == 0), stop=(g == 1),
+                    )
+
+        def ja(G, h, eng):
+            x = work.tile([128, 4, 512], F32, name="ja", tag="ja", bufs=2, align_bytes=64)
+            held["ja", G, h] = x
+            for t in range(4):
+                src = jn_raw[G][:, t, 512 * h:512 * (h + 1)]
+                if eng is V:
+                    nc.vector.tensor_scalar(out=x[:, t, :], in0=src, scalar1=act32[:, G, t:t + 1], scalar2=None, op0=MULT)
+                else:
+                    nc.scalar.activation(out=x[:, t, :], in_=src, func=COPY, scale=act32[:, G, t:t + 1])
+
+        def stt(G, h):
+            x = work.tile([128, 4, 512], BF16, name="jac", tag="jac", bufs=2, align_bytes=64)
+            held["jac", G, h] = x
+            for t in range(4):
+                nc.vector.scalar_tensor_tensor(
+                    out=x[:, t, :], in0=held["corr", G, h, t][:], scalar=act32[:, G, t:t + 1],
+                    in1=held["ja", G, h][:, t, :], op0=MULT, op1=ADD)
+
+        def il_jac(G, h, eng):
+            interleave(eng, ("gjac", G, h), held["jac", G, h][:])
+
+        def q_jac(G, h):
+            cols = slice(512 * h, 512 * (h + 1))
+            quantize(("gjac", G, h), jac_c[:, G, cols], jac_s[:, G, cols])
+
+        def flip_rows(key, half, pr, words, first):
+            x = bank(key + (pr,))
+            x4 = x[:].rearrange("p (j u m) -> p j u m", j=2, u=2)
+            for j in range(2):
+                for u in range(2):
+                    nc.tensor.transpose(x4[:, j, u, :], words[:, first + j, half + u:half + 256:2], ident[:])
+
+        def exit_rows(key, pr):
+            if pr == 0:
+                grp_tile(key)
+            x4 = held[key + (pr,)][:].rearrange("p (j u m) -> p j u m", j=2, u=2)
+            dst = held[key][:].rearrange("p n t -> p (n t)").bitcast(F32).rearrange("p (j m u) -> p j m u", j=4, u=2)
+            nc.scalar.copy(out=dst[:, 2 * pr:2 * pr + 2, :, :], in_=x4.rearrange("p j u m -> p j m u"))
+
+        def flip_force(jh, G):
+            for pr in range(2):
+                flip_rows(("f", jh, G), 256 * G, pr, f_raw[2 * jh + pr][:].bitcast(F32), 0)
+
+        def exit_force(jh, G):
+            for pr in range(2):
+                exit_rows(("f", jh, G), pr)
+
+        def exit_pose(jh):
+            for pr in range(2):
+                exit_rows(("p", jh), pr)
+
+        def q_force(jh, G):
+            cols = slice(512 * jh, 512 * (jh + 1))
+            quantize(("f", jh, G), f_c[:, G, cols], f_s[:, G, cols])
+
+        def flip_pose(jh):
+            for pr in range(2):
+                flip_rows(("p", jh), 0, pr, raw["p", jh][:].bitcast(F32), 2 * pr)
+
+        def q_pose(jh):
+            cols = slice(512 * jh, 512 * (jh + 1))
+            quantize(("p", jh), p_c[:, cols], p_s[:, cols])
+
+        def mm2_pass(j, h, lc, ls, rc, rs, start, stop):
+            rows = slice(128 * j, 128 * (j + 1))
+            cols = slice(512 * h, 512 * (h + 1))
+            nc.tensor.matmul_mx(
+                out=held["o", j, h][:], lhsT=lc[:, rows].bitcast(FP8X4), lhsT_scale=ls[:, rows],
+                rhs=rc[:, cols].bitcast(FP8X4), rhs_scale=rs[:, cols], start=start, stop=stop)
+
+        def mm2(j, h, G):
+            if G < 0:
+                bank(("o", j, h))
+                mm2_pass(j, h, p_c, p_s, wg_c, wg_s, True, False)
+            else:
+                mm2_pass(j, h, f_c[:, G, :], f_s[:, G, :], jac_c[:, G, :], jac_s[:, G, :], False, G == 2)
+
+        def store(j, h, eng):
+            x = work.tile([128, 512], F32, name="o_sb", tag="o_sb", bufs=5, align_bytes=64)
+            copy_on(eng, x[:], held["o", j, h][:])
+            nc.sync.dma_start(out=out_v[j][:, 512 * h:512 * (h + 1)], in_=x[:])
+
+
+        ld_w(0, 0)
+        ld_phi(0)
+        ld_w(1, 0)
+        ld_phi(1)
+        ld_jn(0)
+        ld_phi(2)
+        ld_jn(1)
+        ld_w(1, 1)
+        ld_w(0, 1)
+        ld_force(0)
+        ld_force(1)
+        ld_jn(2)
+        ld_pose(0)
+        ld_force(2)
+        ld_force(3)
+        il_w(0, 0, V)
+        cast_act()
+        il_w(1, 0, S)
+        ld_wg(0)
+        ld_pose(1)
+        q_w(0, 0)
+        prod(0, 3)
+        flip_phi(0, 3)
+        prod(0, 1)
+        flip_phi(0, 1)
+        prod(1, 3)
+        prod(1, 1)
+        exit_phi(0, 1)
+        prod(0, 2)
+        ja(0, 0, S)
+        prod(1, 0)
+        exit_phi(0, 3)
+        flip_phi(1, 3)
+        flip_phi(0, 2)
+        flip_phi(1, 1)
+        exit_phi(1, 1)
+        flip_phi(1, 0)
+        prod(0, 0)
+        flip_phi(0, 0)
+        prod(1, 2)
+        flip_phi(1, 2)
+        flip_force(0, 1)
+        ja(1, 0, S)
+        exit_phi(0, 2)
+        exit_phi(0, 0)
+        prod(2, 1)
+        il_w(0, 1, V)
+        exit_phi(1, 2)
+        q_w(1, 0)
+        q_phi(0)
+        mm1(0, 0)
+        exit_phi(1, 3)
+        prod(2, 3)
+        prod(2, 0)
+        exit_phi(1, 0)
+        exit_force(0, 1)
+        q_phi(1)
+        q_force(0, 1)
+        flip_force(0, 2)
+        il_w(1, 1, S)
+        ld_wg(1)
+        flip_force(0, 0)
+        exit_force(0, 2)
+        stt(0, 0)
+        prod(2, 2)
+        flip_phi(2, 3)
+        mm1(1, 0)
+        q_w(0, 1)
+        flip_phi(2, 2)
+        flip_force(1, 0)
+        exit_force(0, 0)
+        il_jac(0, 0, S)
+        exit_phi(2, 3)
+        stt(1, 0)
+        exit_force(1, 0)
+        q_w(1, 1)
+        flip_phi(2, 1)
+        exit_phi(2, 1)
+        exit_phi(2, 2)
+        ja(2, 0, V)
+        q_force(0, 0)
+        q_force(1, 0)
+        flip_pose(0)
+        flip_phi(2, 0)
+        exit_phi(2, 0)
+        flip_pose(1)
+        exit_pose(1)
+        q_phi(2)
+        il_wg(0, S)
+        mm1(2, 0)
+        exit_pose(0)
+        q_jac(0, 0)
+        q_force(0, 2)
+        stt(2, 0)
+        ja(0, 1, S)
+        q_pose(1)
+        il_jac(1, 0, V)
+        q_wg(0)
+        flip_force(1, 1)
+        exit_force(1, 1)
+        flip_force(1, 2)
+        mm1(0, 1)
+        exit_force(1, 2)
+        q_pose(0)
+        q_jac(1, 0)
+        il_jac(2, 0, V)
+        mm2(0, 0, -1)
+        mm2(0, 0, 0)
+        mm2(0, 0, 1)
+        mm1(1, 1)
+        mm2(2, 0, -1)
+        mm2(2, 0, 0)
+        mm2(2, 0, 1)
+        stt(0, 1)
+        mm2(3, 0, -1)
+        mm2(3, 0, 0)
+        ja(1, 1, S)
+        mm2(1, 0, -1)
+        mm2(3, 0, 1)
+        q_jac(2, 0)
+        mm2(1, 0, 0)
+        mm2(0, 0, 2)
+        q_force(1, 2)
+        il_wg(1, S)
+        mm2(1, 0, 1)
+        mm2(1, 0, 2)
+        store(0, 0, S)
+        mm2(3, 0, 2)
+        mm2(2, 0, 2)
+        store(2, 0, S)
+        mm1(2, 1)
+        store(1, 0, S)
+        store(3, 0, S)
+        mm2(6, 0, -1)
+        mm2(6, 0, 0)
+        q_wg(1)
+        stt(1, 1)
+        ja(2, 1, S)
+        q_force(1, 1)
+        mm2(6, 0, 1)
+        mm2(6, 0, 2)
+        mm2(4, 0, -1)
+        mm2(5, 0, -1)
+        mm2(5, 0, 0)
+        mm2(4, 0, 0)
+        il_jac(1, 1, S)
+        mm2(5, 0, 1)
+        mm2(7, 0, -1)
+        mm2(5, 0, 2)
+        il_jac(0, 1, V)
+        stt(2, 1)
+        mm2(4, 0, 1)
+        mm2(4, 0, 2)
+        q_jac(0, 1)
+        store(6, 0, V)
+        mm2(7, 0, 0)
+        mm2(1, 1, -1)
+        mm2(4, 1, -1)
+        mm2(2, 1, -1)
+        mm2(7, 0, 1)
+        mm2(7, 0, 2)
+        mm2(6, 1, -1)
+        mm2(6, 1, 0)
+        mm2(1, 1, 0)
+        q_jac(1, 1)
+        il_jac(2, 1, S)
+        mm2(3, 1, -1)
+        mm2(3, 1, 0)
+        mm2(3, 1, 1)
+        store(7, 0, S)
+        mm2(4, 1, 0)
+        store(4, 0, V)
+        mm2(2, 1, 0)
+        mm2(6, 1, 1)
+        mm2(1, 1, 1)
+        mm2(2, 1, 1)
+        q_jac(2, 1)
+        mm2(3, 1, 2)
+        store(5, 0, V)
+        mm2(2, 1, 2)
+        store(3, 1, V)
+        mm2(5, 1, -1)
+        mm2(6, 1, 2)
+        mm2(0, 1, -1)
+        mm2(7, 1, -1)
+        store(6, 1, S)
+        mm2(7, 1, 0)
+        mm2(7, 1, 1)
+        mm2(7, 1, 2)
+        mm2(1, 1, 2)
+        mm2(0, 1, 0)
+        store(2, 1, V)
+        store(7, 1, V)
+        mm2(0, 1, 1)
+        mm2(0, 1, 2)
+        mm2(5, 1, 0)
+        mm2(5, 1, 1)
+        mm2(5, 1, 2)
+        store(1, 1, S)
+        store(0, 1, S)
+        store(5, 1, S)
+        mm2(4, 1, 1)
+        mm2(4, 1, 2)
+        store(4, 1, V)

@@ -21,6 +21,7 @@ def tile_contact_jacobian_torque_s7_kernel(tc, phi_bytes, phi_scale, w, j_nom, a
     nc = tc.nc
     V = nc.vector
     S = nc.scalar
+    GP = nc.gpsimd
     with ExitStack() as ctx:
         keep = ctx.enter_context(tc.tile_pool(name="keep", bufs=1))
         work = ctx.enter_context(tc.tile_pool(name="work", bufs=1))
@@ -29,6 +30,8 @@ def tile_contact_jacobian_torque_s7_kernel(tc, phi_bytes, phi_scale, w, j_nom, a
 
         ident = keep.tile([128, 128], F32, name="ident")
         make_identity(nc, ident[:])
+        ident16 = keep.tile([128, 128], BF16, name="ident16")
+        make_identity(nc, ident16[:])
 
         scale = keep.tile([128, K], F32, name="scale")
         nc.scalar.dma_start(out=scale[:], in_=phi_scale.rearrange("o k -> (o k)").partition_broadcast(128))
@@ -53,7 +56,7 @@ def tile_contact_jacobian_torque_s7_kernel(tc, phi_bytes, phi_scale, w, j_nom, a
             return t
 
         phi_raw = {}
-        jn_raw = [work.tile([128, 4, D], BF16, name="jn_raw%d" % g, tag="jn_raw", bufs=3, align_bytes=64) for g in range(3)]
+        jn_raw = {}
         f_raw = [work.tile([128, 2, C], BF16, name="f_raw%d" % i, tag="f_raw", bufs=4, align_bytes=64) for i in range(4)]
 
         def ld_w(g, h):
@@ -64,8 +67,10 @@ def tile_contact_jacobian_torque_s7_kernel(tc, phi_bytes, phi_scale, w, j_nom, a
             phi_raw[G] = work.tile([128, 4, K], U8, name="phi_raw", tag="phi_raw", bufs=3, align_bytes=64)
             nc.sync.dma_start(out=phi_raw[G][:], in_=phi_v[G])
 
-        def ld_jn(G):
-            nc.sync.dma_start(out=jn_raw[G][:], in_=jn_v[G])
+        def ld_jn(G, h):
+            x = work.tile([128, 4, 512], BF16, name="jn_raw", tag="jn_raw", bufs=6, align_bytes=64)
+            jn_raw[G, h] = x
+            nc.sync.dma_start(out=x[:], in_=jn_v[G][:, :, 512 * h:512 * (h + 1)])
 
         def ld_force(i):
             nc.sync.dma_start(out=f_raw[i][:], in_=force_v[:, 2 * i:2 * i + 2, :])
@@ -96,12 +101,12 @@ def tile_contact_jacobian_torque_s7_kernel(tc, phi_bytes, phi_scale, w, j_nom, a
         wg_s = keep.tile([128, D], U8, name="wg_s", align_bytes=64)
 
         def grp_tile(key):
-            t = work.tile([128, 512, 4], BF16, name="grp", tag="grp", bufs=6, align_bytes=64)
+            t = work.tile([128, 512, 4], BF16, name="grp", tag="grp", bufs=7, align_bytes=64)
             held[key] = t
             return t
 
-        def bank(key):
-            t = psum.tile([128, 512], F32, name="bank", tag="bank", bufs=8)
+        def bank(key, ring, dtype=F32):
+            t = psum.tile([128, 2048 // (4 if dtype == F32 else 2)], dtype, name="bank_" + ring, tag="bank_" + ring, bufs=4)
             held[key] = t
             return t
 
@@ -117,6 +122,23 @@ def tile_contact_jacobian_torque_s7_kernel(tc, phi_bytes, phi_scale, w, j_nom, a
 
         def quantize(key, codes, scales):
             nc.vector.quantize_mx(out=codes.bitcast(FP8X4), scales=scales, in_=held[key][:].rearrange("p n t -> p (n t)"))
+
+        def planes(kind, *key):
+            return raw[(kind,) + key][:] if kind != "jac" else held[(kind,) + key][:]
+
+        def pil(*key):
+            src = planes(*key)
+            for i in range(2):
+                x = bank(("il", i) + key, "a", BF16)
+                for half in range(2):
+                    c0 = 256 * i + 128 * half
+                    nc.tensor.matmul(x[:, 512 * half:512 * (half + 1)], ident16[:], src[:, :, c0:c0 + 128].rearrange("p t c -> p c t"), start=True, stop=True)
+
+        def pex(eng, *key):
+            t = grp_tile(("gjac",) + key[1:] if key[0] == "jac" else key)
+            dst = t[:].rearrange("p n t -> p (n t)").bitcast(F32)
+            for i in range(2):
+                copy_on(eng, dst[:, 512 * i:512 * (i + 1)], held[("il", i) + key][:].bitcast(F32))
 
         def il_w(g, h, eng):
             interleave(eng, ("w", g, h), raw["w", g, h][:])
@@ -139,7 +161,7 @@ def tile_contact_jacobian_torque_s7_kernel(tc, phi_bytes, phi_scale, w, j_nom, a
 
         def flip_phi(G, t):
             words = held["ph", G, t][:].bitcast(F32)
-            x = bank(("flip", G, t))
+            x = bank(("flip", G, t), "a")
             x4 = x[:].rearrange("p (g u m) -> p g u m", g=2, u=2)
             for g in range(2):
                 for u in range(2):
@@ -162,7 +184,7 @@ def tile_contact_jacobian_torque_s7_kernel(tc, phi_bytes, phi_scale, w, j_nom, a
         def mm1(G, h):
             cols = slice(512 * h, 512 * (h + 1))
             for t in range(4):
-                x = bank(("corr", G, h, t))
+                x = bank(("corr", G, h, t), "b")
                 for g in range(2):
                     nc.tensor.matmul_mx(
                         out=x[:],
@@ -174,14 +196,16 @@ def tile_contact_jacobian_torque_s7_kernel(tc, phi_bytes, phi_scale, w, j_nom, a
                     )
 
         def ja(G, h, eng):
-            x = work.tile([128, 4, 512], F32, name="ja", tag="ja", bufs=2, align_bytes=64)
-            held["ja", G, h] = x
             for t in range(4):
-                src = jn_raw[G][:, t, 512 * h:512 * (h + 1)]
+                x = work.tile([128, 512], F32, name="ja", tag="ja", bufs=8, align_bytes=64)
+                held["ja", G, h, t] = x
+                src = jn_raw[G, h][:, t, :]
                 if eng is V:
-                    nc.vector.tensor_scalar(out=x[:, t, :], in0=src, scalar1=act32[:, G, t:t + 1], scalar2=None, op0=MULT)
+                    nc.vector.tensor_scalar(out=x[:], in0=src, scalar1=act32[:, G, t:t + 1], scalar2=None, op0=MULT)
+                elif eng is GP:
+                    nc.gpsimd.tensor_scalar(out=x[:], in0=src, scalar1=act32[:, G, t:t + 1], scalar2=0.0, op0=MULT, op1=ADD)
                 else:
-                    nc.scalar.activation(out=x[:, t, :], in_=src, func=COPY, scale=act32[:, G, t:t + 1])
+                    nc.scalar.activation(out=x[:], in_=src, func=COPY, scale=act32[:, G, t:t + 1])
 
         def stt(G, h):
             x = work.tile([128, 4, 512], BF16, name="jac", tag="jac", bufs=2, align_bytes=64)
@@ -189,7 +213,7 @@ def tile_contact_jacobian_torque_s7_kernel(tc, phi_bytes, phi_scale, w, j_nom, a
             for t in range(4):
                 nc.vector.scalar_tensor_tensor(
                     out=x[:, t, :], in0=held["corr", G, h, t][:], scalar=act32[:, G, t:t + 1],
-                    in1=held["ja", G, h][:, t, :], op0=MULT, op1=ADD)
+                    in1=held["ja", G, h, t][:], op0=MULT, op1=ADD)
 
         def il_jac(G, h, eng):
             interleave(eng, ("gjac", G, h), held["jac", G, h][:])
@@ -199,7 +223,7 @@ def tile_contact_jacobian_torque_s7_kernel(tc, phi_bytes, phi_scale, w, j_nom, a
             quantize(("gjac", G, h), jac_c[:, G, cols], jac_s[:, G, cols])
 
         def flip_rows(key, half, pr, words, first):
-            x = bank(key + (pr,))
+            x = bank(key + (pr,), "a")
             x4 = x[:].rearrange("p (j u m) -> p j u m", j=2, u=2)
             for j in range(2):
                 for u in range(2):
@@ -245,7 +269,7 @@ def tile_contact_jacobian_torque_s7_kernel(tc, phi_bytes, phi_scale, w, j_nom, a
 
         def mm2(j, h, G):
             if G < 0:
-                bank(("o", j, h))
+                bank(("o", j, h), "b" if h == 1 and j % 2 == 1 else "a")
                 mm2_pass(j, h, p_c, p_s, wg_c, wg_s, True, False)
             else:
                 mm2_pass(j, h, f_c[:, G, :], f_s[:, G, :], jac_c[:, G, :], jac_s[:, G, :], False, G == 2)
@@ -256,207 +280,210 @@ def tile_contact_jacobian_torque_s7_kernel(tc, phi_bytes, phi_scale, w, j_nom, a
             nc.sync.dma_start(out=out_v[j][:, 512 * h:512 * (h + 1)], in_=x[:])
 
 
+        cast_act()
         ld_w(0, 0)
+        il_w(0, 0, V)
         ld_phi(0)
         ld_w(1, 0)
         ld_phi(1)
-        ld_jn(0)
-        ld_phi(2)
-        ld_jn(1)
-        ld_w(1, 1)
-        ld_w(0, 1)
-        ld_force(0)
-        ld_force(1)
-        ld_jn(2)
-        ld_pose(0)
-        ld_force(2)
-        ld_force(3)
-        il_w(0, 0, V)
-        cast_act()
-        il_w(1, 0, S)
-        ld_wg(0)
-        ld_pose(1)
         q_w(0, 0)
-        prod(0, 3)
-        flip_phi(0, 3)
-        prod(0, 1)
-        flip_phi(0, 1)
-        prod(1, 3)
-        prod(1, 1)
-        exit_phi(0, 1)
+        ld_pose(0)
+        il_w(1, 0, S)
         prod(0, 2)
-        ja(0, 0, S)
-        prod(1, 0)
-        exit_phi(0, 3)
-        flip_phi(1, 3)
         flip_phi(0, 2)
-        flip_phi(1, 1)
-        exit_phi(1, 1)
-        flip_phi(1, 0)
-        prod(0, 0)
-        flip_phi(0, 0)
-        prod(1, 2)
-        flip_phi(1, 2)
-        flip_force(0, 1)
-        ja(1, 0, S)
         exit_phi(0, 2)
-        exit_phi(0, 0)
-        prod(2, 1)
-        il_w(0, 1, V)
-        exit_phi(1, 2)
-        q_w(1, 0)
-        q_phi(0)
-        mm1(0, 0)
-        exit_phi(1, 3)
-        prod(2, 3)
-        prod(2, 0)
-        exit_phi(1, 0)
-        exit_force(0, 1)
-        q_phi(1)
-        q_force(0, 1)
-        flip_force(0, 2)
-        il_w(1, 1, S)
-        ld_wg(1)
-        flip_force(0, 0)
-        exit_force(0, 2)
-        stt(0, 0)
-        prod(2, 2)
-        flip_phi(2, 3)
-        mm1(1, 0)
-        q_w(0, 1)
-        flip_phi(2, 2)
-        flip_force(1, 0)
-        exit_force(0, 0)
-        il_jac(0, 0, S)
-        exit_phi(2, 3)
-        stt(1, 0)
-        exit_force(1, 0)
-        q_w(1, 1)
-        flip_phi(2, 1)
-        exit_phi(2, 1)
-        exit_phi(2, 2)
-        ja(2, 0, V)
-        q_force(0, 0)
-        q_force(1, 0)
+        prod(0, 0)
+        ld_force(0)
         flip_pose(0)
-        flip_phi(2, 0)
-        exit_phi(2, 0)
-        flip_pose(1)
-        exit_pose(1)
-        q_phi(2)
-        il_wg(0, S)
-        mm1(2, 0)
+        ld_force(1)
+        flip_phi(0, 0)
+        prod(0, 1)
+        prod(1, 3)
+        exit_phi(0, 0)
+        flip_phi(1, 3)
+        prod(0, 3)
+        flip_phi(0, 1)
         exit_pose(0)
-        q_jac(0, 0)
-        q_force(0, 2)
-        stt(2, 0)
-        ja(0, 1, S)
-        q_pose(1)
-        il_jac(1, 0, V)
-        q_wg(0)
-        flip_force(1, 1)
-        exit_force(1, 1)
-        flip_force(1, 2)
-        mm1(0, 1)
-        exit_force(1, 2)
+        prod(1, 1)
+        ld_phi(2)
+        prod(1, 2)
+        ld_jn(2, 0)
+        prod(1, 0)
+        ld_jn(0, 0)
+        flip_phi(0, 3)
+        exit_phi(0, 1)
+        prod(2, 0)
+        flip_force(0, 2)
+        exit_phi(1, 3)
+        flip_phi(1, 1)
+        prod(2, 2)
+        flip_phi(1, 2)
+        exit_phi(0, 3)
+        ld_w(0, 1)
+        prod(2, 3)
+        ld_pose(1)
+        flip_phi(1, 0)
+        exit_force(0, 2)
+        prod(2, 1)
+        q_w(1, 0)
+        ld_jn(1, 0)
+        ld_wg(0)
+        flip_force(0, 0)
+        exit_phi(1, 2)
+        exit_phi(1, 1)
+        flip_force(0, 1)
+        flip_phi(2, 0)
+        flip_phi(2, 3)
+        q_phi(0)
+        exit_phi(1, 0)
+        ld_force(3)
+        flip_phi(2, 1)
+        flip_phi(2, 2)
+        q_phi(1)
+        exit_force(0, 0)
+        mm1(0, 0)
+        ld_w(1, 1)
+        exit_force(0, 1)
+        ja(0, 0, GP)
+        il_w(0, 1, S)
+        mm1(1, 0)
+        ja(1, 0, GP)
+        ld_force(2)
+        ld_jn(0, 1)
+        stt(0, 0)
+        exit_phi(2, 3)
+        flip_pose(1)
+        ja(0, 1, GP)
         q_pose(0)
-        q_jac(1, 0)
-        il_jac(2, 0, V)
+        exit_phi(2, 0)
+        q_force(0, 2)
+        exit_phi(2, 2)
+        flip_force(1, 2)
+        exit_phi(2, 1)
+        q_phi(2)
+        stt(1, 0)
+        il_wg(0, S)
+        q_force(0, 0)
+        ja(2, 0, GP)
+        q_w(0, 1)
+        q_force(0, 1)
+        q_wg(0)
+        mm1(2, 0)
+        flip_force(1, 0)
+        flip_force(1, 1)
+        il_w(1, 1, V)
+        il_jac(0, 0, S)
         mm2(0, 0, -1)
-        mm2(0, 0, 0)
-        mm2(0, 0, 1)
-        mm1(1, 1)
         mm2(2, 0, -1)
-        mm2(2, 0, 0)
-        mm2(2, 0, 1)
-        stt(0, 1)
-        mm2(3, 0, -1)
-        mm2(3, 0, 0)
-        ja(1, 1, S)
         mm2(1, 0, -1)
-        mm2(3, 0, 1)
-        q_jac(2, 0)
+        ld_jn(1, 1)
+        exit_pose(1)
+        q_jac(0, 0)
+        mm2(2, 0, 0)
+        exit_force(1, 2)
+        mm2(3, 0, -1)
         mm2(1, 0, 0)
-        mm2(0, 0, 2)
-        q_force(1, 2)
+        mm2(0, 0, 0)
+        mm2(3, 0, 0)
+        ld_wg(1)
+        q_w(1, 1)
+        stt(2, 0)
+        exit_force(1, 0)
+        mm1(0, 1)
+        exit_force(1, 1)
+        il_jac(1, 0, S)
+        il_jac(2, 0, S)
+        q_jac(1, 0)
         il_wg(1, S)
+        stt(0, 1)
         mm2(1, 0, 1)
+        q_jac(2, 0)
+        mm2(3, 0, 1)
+        mm2(0, 0, 1)
+        q_pose(1)
+        mm1(1, 1)
+        ja(1, 1, GP)
+        mm2(2, 0, 1)
+        ld_jn(2, 1)
+        ja(2, 1, GP)
+        mm2(0, 0, 2)
         mm2(1, 0, 2)
-        store(0, 0, S)
+        stt(1, 1)
         mm2(3, 0, 2)
         mm2(2, 0, 2)
-        store(2, 0, S)
         mm1(2, 1)
-        store(1, 0, S)
-        store(3, 0, S)
         mm2(6, 0, -1)
+        mm2(5, 0, -1)
+        q_force(1, 0)
+        mm2(5, 0, 0)
+        q_force(1, 2)
+        store(1, 0, S)
         mm2(6, 0, 0)
-        q_wg(1)
-        stt(1, 1)
-        ja(2, 1, S)
         q_force(1, 1)
+        mm2(4, 0, -1)
         mm2(6, 0, 1)
         mm2(6, 0, 2)
-        mm2(4, 0, -1)
-        mm2(5, 0, -1)
-        mm2(5, 0, 0)
-        mm2(4, 0, 0)
-        il_jac(1, 1, S)
+        store(2, 0, S)
         mm2(5, 0, 1)
         mm2(7, 0, -1)
-        mm2(5, 0, 2)
-        il_jac(0, 1, V)
-        stt(2, 1)
-        mm2(4, 0, 1)
-        mm2(4, 0, 2)
-        q_jac(0, 1)
-        store(6, 0, V)
+        store(3, 0, V)
+        mm2(4, 0, 0)
+        store(0, 0, S)
+        q_wg(1)
+        il_jac(0, 1, S)
+        store(6, 0, S)
         mm2(7, 0, 0)
-        mm2(1, 1, -1)
-        mm2(4, 1, -1)
-        mm2(2, 1, -1)
+        il_jac(1, 1, S)
+        mm2(4, 0, 1)
         mm2(7, 0, 1)
+        q_jac(0, 1)
+        stt(2, 1)
+        mm2(4, 1, -1)
         mm2(7, 0, 2)
-        mm2(6, 1, -1)
-        mm2(6, 1, 0)
-        mm2(1, 1, 0)
-        q_jac(1, 1)
-        il_jac(2, 1, S)
-        mm2(3, 1, -1)
-        mm2(3, 1, 0)
-        mm2(3, 1, 1)
+        mm2(4, 0, 2)
         store(7, 0, S)
-        mm2(4, 1, 0)
-        store(4, 0, V)
-        mm2(2, 1, 0)
-        mm2(6, 1, 1)
-        mm2(1, 1, 1)
-        mm2(2, 1, 1)
-        q_jac(2, 1)
-        mm2(3, 1, 2)
-        store(5, 0, V)
-        mm2(2, 1, 2)
-        store(3, 1, V)
-        mm2(5, 1, -1)
-        mm2(6, 1, 2)
-        mm2(0, 1, -1)
         mm2(7, 1, -1)
-        store(6, 1, S)
+        mm2(5, 1, -1)
+        q_jac(1, 1)
+        mm2(5, 0, 2)
+        mm2(1, 1, -1)
+        store(4, 0, S)
+        mm2(1, 1, 0)
+        mm2(3, 1, -1)
         mm2(7, 1, 0)
-        mm2(7, 1, 1)
-        mm2(7, 1, 2)
-        mm2(1, 1, 2)
-        mm2(0, 1, 0)
-        store(2, 1, V)
-        store(7, 1, V)
-        mm2(0, 1, 1)
-        mm2(0, 1, 2)
+        mm2(3, 1, 0)
         mm2(5, 1, 0)
+        mm2(3, 1, 1)
+        mm2(1, 1, 1)
+        mm2(7, 1, 1)
+        il_jac(2, 1, V)
+        q_jac(2, 1)
         mm2(5, 1, 1)
+        store(5, 0, S)
+        mm2(2, 1, -1)
+        mm2(2, 1, 0)
+        mm2(1, 1, 2)
+        mm2(3, 1, 2)
+        mm2(4, 1, 0)
+        store(3, 1, V)
+        mm2(2, 1, 1)
+        mm2(2, 1, 2)
         mm2(5, 1, 2)
-        store(1, 1, S)
-        store(0, 1, S)
-        store(5, 1, S)
+        mm2(0, 1, -1)
+        store(1, 1, V)
         mm2(4, 1, 1)
+        store(2, 1, V)
+        mm2(7, 1, 2)
         mm2(4, 1, 2)
+        store(5, 1, S)
+        mm2(0, 1, 0)
+        mm2(6, 1, -1)
+        mm2(0, 1, 1)
+        store(7, 1, V)
+        mm2(0, 1, 2)
         store(4, 1, V)
+        mm2(6, 1, 0)
+        store(0, 1, S)
+        mm2(6, 1, 1)
+        mm2(6, 1, 2)
+        store(6, 1, S)

@@ -28,16 +28,16 @@ def tile_contact_jacobian_torque_s7_kernel(tc, phi_bytes, phi_scale, w, j_nom, a
         psum = ctx.enter_context(tc.psum_pool(name="psum", bufs=8))
         ctx.enter_context(tc.manual_schedule())
 
+        zeros = keep.tile([128, 512], BF16, name="zeros", align_bytes=64)
+        nc.gpsimd.memset(zeros[:], 0.0)
         ident = keep.tile([128, 128], F32, name="ident")
         make_identity(nc, ident[:])
-        ident16 = keep.tile([128, 128], BF16, name="ident16")
-        make_identity(nc, ident16[:])
-
         scale = keep.tile([128, K], F32, name="scale")
         nc.scalar.dma_start(out=scale[:], in_=phi_scale.rearrange("o k -> (o k)").partition_broadcast(128))
         act16 = keep.tile([128, 3, 4], BF16, name="act16")
-        nc.scalar.dma_start(out=act16[:], in_=act.rearrange("(g p t) -> p g t", p=128, t=4))
+        nc.gpsimd.dma_start(out=act16[:], in_=act.rearrange("(g p t) -> p g t", p=128, t=4))
         act32 = keep.tile([128, 3, 4], F32, name="act32")
+        nc.gpsimd.tensor_copy(out=act32[:], in_=act16[:])
 
         held = {}
         w_v = w.rearrange("(g p t) n -> g p t n", p=128, t=4)
@@ -83,9 +83,6 @@ def tile_contact_jacobian_torque_s7_kernel(tc, phi_bytes, phi_scale, w, j_nom, a
             x = raw_tile(("p", jh))
             nc.sync.dma_start(out=x[:], in_=pose_v[:, 4 * jh:4 * jh + 4, :])
 
-        def cast_act():
-            nc.vector.tensor_copy(out=act32[:], in_=act16[:])
-
 
         phi_c = keep.tile([128, 3, 2, 512], U32, name="phi_c", align_bytes=64)
         phi_s = keep.tile([128, 3, 2, 512], U8, name="phi_s", align_bytes=64)
@@ -110,6 +107,11 @@ def tile_contact_jacobian_torque_s7_kernel(tc, phi_bytes, phi_scale, w, j_nom, a
             held[key] = t
             return t
 
+        def warm(i):
+            x = bank(("warm", i), "b")
+            for k in range(2):
+                nc.tensor.matmul(x[:], zeros[:, 0:128], zeros[:], start=True, stop=True)
+
         def copy_on(eng, dst, src):
             if eng is V:
                 nc.vector.tensor_copy(out=dst, in_=src)
@@ -122,23 +124,6 @@ def tile_contact_jacobian_torque_s7_kernel(tc, phi_bytes, phi_scale, w, j_nom, a
 
         def quantize(key, codes, scales):
             nc.vector.quantize_mx(out=codes.bitcast(FP8X4), scales=scales, in_=held[key][:].rearrange("p n t -> p (n t)"))
-
-        def planes(kind, *key):
-            return raw[(kind,) + key][:] if kind != "jac" else held[(kind,) + key][:]
-
-        def pil(*key):
-            src = planes(*key)
-            for i in range(2):
-                x = bank(("il", i) + key, "a", BF16)
-                for half in range(2):
-                    c0 = 256 * i + 128 * half
-                    nc.tensor.matmul(x[:, 512 * half:512 * (half + 1)], ident16[:], src[:, :, c0:c0 + 128].rearrange("p t c -> p c t"), start=True, stop=True)
-
-        def pex(eng, *key):
-            t = grp_tile(("gjac",) + key[1:] if key[0] == "jac" else key)
-            dst = t[:].rearrange("p n t -> p (n t)").bitcast(F32)
-            for i in range(2):
-                copy_on(eng, dst[:, 512 * i:512 * (i + 1)], held[("il", i) + key][:].bitcast(F32))
 
         def il_w(g, h, eng):
             interleave(eng, ("w", g, h), raw["w", g, h][:])
@@ -280,210 +265,218 @@ def tile_contact_jacobian_torque_s7_kernel(tc, phi_bytes, phi_scale, w, j_nom, a
             nc.sync.dma_start(out=out_v[j][:, 512 * h:512 * (h + 1)], in_=x[:])
 
 
-        cast_act()
+        warm(0)
+        warm(1)
         ld_w(0, 0)
-        il_w(0, 0, V)
+        warm(2)
+        ld_wg(0)
         ld_phi(0)
+        il_w(0, 0, V)
         ld_w(1, 0)
         ld_phi(1)
         q_w(0, 0)
-        ld_pose(0)
-        il_w(1, 0, S)
-        prod(0, 2)
-        flip_phi(0, 2)
-        exit_phi(0, 2)
-        prod(0, 0)
-        ld_force(0)
-        flip_pose(0)
-        ld_force(1)
-        flip_phi(0, 0)
-        prod(0, 1)
-        prod(1, 3)
-        exit_phi(0, 0)
-        flip_phi(1, 3)
-        prod(0, 3)
-        flip_phi(0, 1)
-        exit_pose(0)
-        prod(1, 1)
-        ld_phi(2)
-        prod(1, 2)
-        ld_jn(2, 0)
-        prod(1, 0)
         ld_jn(0, 0)
-        flip_phi(0, 3)
-        exit_phi(0, 1)
-        prod(2, 0)
-        flip_force(0, 2)
-        exit_phi(1, 3)
-        flip_phi(1, 1)
-        prod(2, 2)
-        flip_phi(1, 2)
-        exit_phi(0, 3)
-        ld_w(0, 1)
-        prod(2, 3)
-        ld_pose(1)
-        flip_phi(1, 0)
-        exit_force(0, 2)
-        prod(2, 1)
-        q_w(1, 0)
         ld_jn(1, 0)
-        ld_wg(0)
-        flip_force(0, 0)
-        exit_phi(1, 2)
-        exit_phi(1, 1)
-        flip_force(0, 1)
-        flip_phi(2, 0)
-        flip_phi(2, 3)
-        q_phi(0)
-        exit_phi(1, 0)
-        ld_force(3)
-        flip_phi(2, 1)
-        flip_phi(2, 2)
-        q_phi(1)
-        exit_force(0, 0)
-        mm1(0, 0)
-        ld_w(1, 1)
-        exit_force(0, 1)
-        ja(0, 0, GP)
-        il_w(0, 1, S)
-        mm1(1, 0)
-        ja(1, 0, GP)
-        ld_force(2)
-        ld_jn(0, 1)
-        stt(0, 0)
-        exit_phi(2, 3)
-        flip_pose(1)
-        ja(0, 1, GP)
-        q_pose(0)
-        exit_phi(2, 0)
-        q_force(0, 2)
-        exit_phi(2, 2)
-        flip_force(1, 2)
-        exit_phi(2, 1)
-        q_phi(2)
-        stt(1, 0)
         il_wg(0, S)
-        q_force(0, 0)
-        ja(2, 0, GP)
-        q_w(0, 1)
-        q_force(0, 1)
-        q_wg(0)
-        mm1(2, 0)
-        flip_force(1, 0)
-        flip_force(1, 1)
-        il_w(1, 1, V)
-        il_jac(0, 0, S)
-        mm2(0, 0, -1)
-        mm2(2, 0, -1)
-        mm2(1, 0, -1)
-        ld_jn(1, 1)
+        prod(0, 0)
+        prod(0, 1)
+        prod(0, 2)
+        flip_phi(0, 0)
+        prod(0, 3)
+        warm(3)
+        flip_phi(0, 2)
+        prod(1, 0)
+        prod(1, 1)
+        il_w(1, 0, S)
+        flip_phi(0, 1)
+        flip_phi(0, 3)
+        warm(4)
+        flip_phi(1, 0)
+        prod(1, 2)
+        warm(5)
+        exit_phi(0, 0)
+        ld_pose(0)
+        ld_phi(2)
+        exit_phi(0, 1)
+        exit_phi(0, 2)
+        flip_pose(0)
+        ld_pose(1)
+        q_w(1, 0)
+        flip_phi(1, 1)
+        exit_phi(0, 3)
+        prod(1, 3)
+        prod(2, 0)
+        prod(2, 1)
+        exit_phi(1, 0)
+        prod(2, 2)
+        ld_force(0)
+        ja(1, 0, S)
+        flip_phi(1, 2)
+        exit_pose(0)
+        warm(6)
+        exit_phi(1, 1)
+        flip_phi(1, 3)
+        flip_pose(1)
+        warm(7)
+        exit_phi(1, 3)
+        ld_force(1)
+        q_phi(0)
+        flip_phi(2, 0)
+        exit_phi(1, 2)
         exit_pose(1)
-        q_jac(0, 0)
-        mm2(2, 0, 0)
-        exit_force(1, 2)
-        mm2(3, 0, -1)
-        mm2(1, 0, 0)
-        mm2(0, 0, 0)
-        mm2(3, 0, 0)
-        ld_wg(1)
-        q_w(1, 1)
-        stt(2, 0)
-        exit_force(1, 0)
-        mm1(0, 1)
-        exit_force(1, 1)
-        il_jac(1, 0, S)
-        il_jac(2, 0, S)
-        q_jac(1, 0)
-        il_wg(1, S)
-        stt(0, 1)
-        mm2(1, 0, 1)
-        q_jac(2, 0)
-        mm2(3, 0, 1)
-        mm2(0, 0, 1)
-        q_pose(1)
-        mm1(1, 1)
-        ja(1, 1, GP)
-        mm2(2, 0, 1)
+        ld_w(0, 1)
+        q_pose(0)
+        flip_phi(2, 2)
+        prod(2, 3)
+        flip_phi(2, 1)
+        ld_jn(2, 0)
+        ld_force(3)
+        ja(0, 0, S)
+        mm1(0, 0)
+        flip_phi(2, 3)
+        q_phi(1)
+        flip_force(0, 0)
+        stt(0, 0)
+        mm1(1, 0)
         ld_jn(2, 1)
-        ja(2, 1, GP)
+        exit_phi(2, 0)
+        exit_phi(2, 1)
+        exit_phi(2, 2)
+        exit_phi(2, 3)
+        il_w(0, 1, S)
+        flip_force(0, 1)
+        ld_w(1, 1)
+        ld_force(2)
+        q_phi(2)
+        exit_force(0, 0)
+        flip_force(0, 2)
+        stt(1, 0)
+        exit_force(0, 1)
+        warm(8)
+        q_pose(1)
+        flip_force(1, 2)
+        ld_jn(1, 1)
+        q_wg(0)
+        q_w(0, 1)
+        flip_force(1, 0)
+        ld_wg(1)
+        il_jac(0, 0, V)
+        exit_force(0, 2)
+        q_force(0, 0)
+        il_w(1, 1, S)
+        q_jac(0, 0)
+        il_jac(1, 0, V)
+        exit_force(1, 0)
+        exit_force(1, 2)
+        ja(2, 0, S)
+        mm1(2, 0)
+        flip_force(1, 1)
+        mm2(0, 0, -1)
+        mm2(0, 0, 0)
+        mm2(2, 0, -1)
+        q_w(1, 1)
+        mm1(0, 1)
+        q_force(0, 1)
+        mm2(2, 0, 0)
+        mm2(1, 0, -1)
+        stt(2, 0)
+        ld_jn(0, 1)
+        mm2(1, 0, 0)
+        exit_force(1, 1)
+        mm2(3, 0, -1)
+        q_jac(1, 0)
+        mm2(3, 0, 0)
+        il_jac(2, 0, V)
+        mm2(2, 0, 1)
+        mm2(0, 0, 1)
+        q_force(0, 2)
+        ja(0, 1, S)
+        mm2(3, 0, 1)
+        q_jac(2, 0)
+        mm2(1, 0, 1)
+        stt(0, 1)
         mm2(0, 0, 2)
+        il_wg(1, S)
+        q_force(1, 0)
         mm2(1, 0, 2)
-        stt(1, 1)
-        mm2(3, 0, 2)
+        q_force(1, 1)
         mm2(2, 0, 2)
         mm1(2, 1)
-        mm2(6, 0, -1)
+        mm2(3, 0, 2)
         mm2(5, 0, -1)
-        q_force(1, 0)
         mm2(5, 0, 0)
-        q_force(1, 2)
-        store(1, 0, S)
-        mm2(6, 0, 0)
-        q_force(1, 1)
+        mm2(6, 0, -1)
         mm2(4, 0, -1)
-        mm2(6, 0, 1)
-        mm2(6, 0, 2)
-        store(2, 0, S)
-        mm2(5, 0, 1)
         mm2(7, 0, -1)
-        store(3, 0, V)
         mm2(4, 0, 0)
         store(0, 0, S)
+        store(2, 0, S)
+        q_force(1, 2)
+        ja(2, 1, V)
+        store(1, 0, S)
         q_wg(1)
-        il_jac(0, 1, S)
-        store(6, 0, S)
+        mm2(5, 0, 1)
         mm2(7, 0, 0)
-        il_jac(1, 1, S)
-        mm2(4, 0, 1)
         mm2(7, 0, 1)
-        q_jac(0, 1)
-        stt(2, 1)
-        mm2(4, 1, -1)
-        mm2(7, 0, 2)
+        mm2(4, 0, 1)
+        store(3, 0, S)
         mm2(4, 0, 2)
-        store(7, 0, S)
-        mm2(7, 1, -1)
-        mm2(5, 1, -1)
-        q_jac(1, 1)
         mm2(5, 0, 2)
+        il_jac(0, 1, S)
+        mm2(6, 0, 0)
+        mm2(6, 0, 1)
+        mm2(6, 0, 2)
+        stt(2, 1)
+        ja(1, 1, S)
+        mm1(1, 1)
         mm2(1, 1, -1)
-        store(4, 0, S)
-        mm2(1, 1, 0)
-        mm2(3, 1, -1)
-        mm2(7, 1, 0)
-        mm2(3, 1, 0)
-        mm2(5, 1, 0)
-        mm2(3, 1, 1)
-        mm2(1, 1, 1)
-        mm2(7, 1, 1)
-        il_jac(2, 1, V)
-        q_jac(2, 1)
-        mm2(5, 1, 1)
+        stt(1, 1)
+        mm2(7, 0, 2)
+        store(6, 0, S)
         store(5, 0, S)
+        mm2(7, 1, -1)
+        mm2(6, 1, -1)
+        q_jac(0, 1)
+        mm2(3, 1, -1)
+        mm2(4, 1, -1)
+        mm2(5, 1, -1)
+        mm2(7, 1, 0)
         mm2(2, 1, -1)
-        mm2(2, 1, 0)
-        mm2(1, 1, 2)
-        mm2(3, 1, 2)
+        store(4, 0, S)
+        il_jac(1, 1, V)
+        mm2(1, 1, 0)
         mm2(4, 1, 0)
-        store(3, 1, V)
+        mm2(0, 1, -1)
+        mm2(0, 1, 0)
+        store(7, 0, S)
+        mm2(6, 1, 0)
+        mm2(5, 1, 0)
+        q_jac(1, 1)
+        il_jac(2, 1, S)
+        q_jac(2, 1)
+        mm2(6, 1, 1)
+        mm2(4, 1, 1)
+        mm2(1, 1, 1)
+        mm2(4, 1, 2)
+        mm2(1, 1, 2)
+        mm2(0, 1, 1)
+        mm2(3, 1, 0)
+        store(4, 1, S)
+        mm2(0, 1, 2)
+        mm2(6, 1, 2)
+        mm2(5, 1, 1)
+        mm2(7, 1, 1)
+        mm2(5, 1, 2)
+        mm2(7, 1, 2)
+        store(1, 1, S)
+        mm2(3, 1, 1)
+        store(0, 1, V)
+        mm2(3, 1, 2)
+        store(6, 1, S)
+        store(5, 1, S)
+        mm2(2, 1, 0)
         mm2(2, 1, 1)
         mm2(2, 1, 2)
-        mm2(5, 1, 2)
-        mm2(0, 1, -1)
-        store(1, 1, V)
-        mm2(4, 1, 1)
-        store(2, 1, V)
-        mm2(7, 1, 2)
-        mm2(4, 1, 2)
-        store(5, 1, S)
-        mm2(0, 1, 0)
-        mm2(6, 1, -1)
-        mm2(0, 1, 1)
         store(7, 1, V)
-        mm2(0, 1, 2)
-        store(4, 1, V)
-        mm2(6, 1, 0)
-        store(0, 1, S)
-        mm2(6, 1, 1)
-        mm2(6, 1, 2)
-        store(6, 1, S)
+        store(3, 1, S)
+        store(2, 1, S)

@@ -21,7 +21,6 @@ def tile_contact_jacobian_torque_s7_kernel(tc, phi_bytes, phi_scale, w, j_nom, a
     nc = tc.nc
     V = nc.vector
     S = nc.scalar
-    GP = nc.gpsimd
     with ExitStack() as ctx:
         keep = ctx.enter_context(tc.tile_pool(name="keep", bufs=1))
         work = ctx.enter_context(tc.tile_pool(name="work", bufs=1))
@@ -33,9 +32,9 @@ def tile_contact_jacobian_torque_s7_kernel(tc, phi_bytes, phi_scale, w, j_nom, a
         ident = keep.tile([128, 128], F32, name="ident")
         make_identity(nc, ident[:])
         scale = keep.tile([128, K], F32, name="scale")
-        nc.scalar.dma_start(out=scale[:], in_=phi_scale.rearrange("o k -> (o k)").partition_broadcast(128))
         act16 = keep.tile([128, 3, 4], BF16, name="act16")
-        nc.gpsimd.dma_start(out=act16[:], in_=act.rearrange("(g p t) -> p g t", p=128, t=4))
+        nc.scalar.dma_start(out=act16[:], in_=act.rearrange("(g p t) -> p g t", p=128, t=4))
+        nc.scalar.dma_start(out=scale[:], in_=phi_scale.rearrange("o k -> (o k)").partition_broadcast(128))
         act32 = keep.tile([128, 3, 4], F32, name="act32")
         nc.gpsimd.tensor_copy(out=act32[:], in_=act16[:])
 
@@ -187,8 +186,6 @@ def tile_contact_jacobian_torque_s7_kernel(tc, phi_bytes, phi_scale, w, j_nom, a
                 src = jn_raw[G, h][:, t, :]
                 if eng is V:
                     nc.vector.tensor_scalar(out=x[:], in0=src, scalar1=act32[:, G, t:t + 1], scalar2=None, op0=MULT)
-                elif eng is GP:
-                    nc.gpsimd.tensor_scalar(out=x[:], in0=src, scalar1=act32[:, G, t:t + 1], scalar2=0.0, op0=MULT, op1=ADD)
                 else:
                     nc.scalar.activation(out=x[:], in_=src, func=COPY, scale=act32[:, G, t:t + 1])
 
@@ -267,216 +264,221 @@ def tile_contact_jacobian_torque_s7_kernel(tc, phi_bytes, phi_scale, w, j_nom, a
 
         warm(0)
         warm(1)
-        ld_w(0, 0)
-        warm(2)
-        ld_wg(0)
-        ld_phi(0)
-        il_w(0, 0, V)
         ld_w(1, 0)
-        ld_phi(1)
-        q_w(0, 0)
-        ld_jn(0, 0)
-        ld_jn(1, 0)
-        il_wg(0, S)
-        prod(0, 0)
-        prod(0, 1)
-        prod(0, 2)
-        flip_phi(0, 0)
-        prod(0, 3)
+        ld_pose(0)
+        warm(2)
         warm(3)
-        flip_phi(0, 2)
+        ld_phi(1)
+        il_w(1, 0, V)
+        flip_pose(0)
+        q_w(1, 0)
         prod(1, 0)
         prod(1, 1)
-        il_w(1, 0, S)
-        flip_phi(0, 1)
-        flip_phi(0, 3)
         warm(4)
         flip_phi(1, 0)
-        prod(1, 2)
-        warm(5)
-        exit_phi(0, 0)
-        ld_pose(0)
-        ld_phi(2)
-        exit_phi(0, 1)
-        exit_phi(0, 2)
-        flip_pose(0)
-        ld_pose(1)
-        q_w(1, 0)
-        flip_phi(1, 1)
-        exit_phi(0, 3)
-        prod(1, 3)
-        prod(2, 0)
-        prod(2, 1)
-        exit_phi(1, 0)
-        prod(2, 2)
-        ld_force(0)
-        ja(1, 0, S)
-        flip_phi(1, 2)
-        exit_pose(0)
-        warm(6)
-        exit_phi(1, 1)
-        flip_phi(1, 3)
-        flip_pose(1)
-        warm(7)
-        exit_phi(1, 3)
-        ld_force(1)
-        q_phi(0)
-        flip_phi(2, 0)
-        exit_phi(1, 2)
-        exit_pose(1)
         ld_w(0, 1)
-        q_pose(0)
-        flip_phi(2, 2)
+        prod(1, 2)
+        ld_phi(0)
+        exit_pose(0)
+        ld_w(0, 0)
+        prod(1, 3)
+        prod(0, 0)
+        ld_force(0)
+        ld_force(1)
+        flip_phi(1, 1)
+        warm(5)
+        il_w(0, 1, S)
+        flip_phi(1, 2)
+        exit_phi(1, 0)
+        exit_phi(1, 1)
+        ld_phi(2)
+        ld_jn(0, 0)
+        prod(0, 1)
+        exit_phi(1, 2)
+        ld_w(1, 1)
+        prod(0, 2)
+        warm(6)
+        flip_phi(1, 3)
+        warm(7)
+        ld_jn(1, 0)
+        flip_phi(0, 0)
+        ld_force(2)
+        il_w(0, 0, S)
+        warm(8)
+        exit_phi(0, 0)
+        ld_pose(1)
+        flip_phi(0, 1)
+        q_w(0, 0)
+        prod(0, 3)
+        exit_phi(1, 3)
+        flip_phi(0, 2)
+        warm(9)
+        prod(2, 0)
+        flip_force(0, 1)
+        exit_phi(0, 2)
+        prod(2, 1)
+        flip_phi(0, 3)
+        warm(10)
+        exit_phi(0, 1)
+        exit_force(0, 1)
+        flip_force(0, 2)
+        exit_phi(0, 3)
+        ld_wg(0)
+        q_phi(0)
+        warm(11)
+        prod(2, 2)
         prod(2, 3)
-        flip_phi(2, 1)
-        ld_jn(2, 0)
-        ld_force(3)
+        flip_force(0, 0)
         ja(0, 0, S)
+        ld_jn(2, 1)
+        ld_force(3)
+        ja(1, 0, S)
         mm1(0, 0)
         flip_phi(2, 3)
-        q_phi(1)
-        flip_force(0, 0)
-        stt(0, 0)
-        mm1(1, 0)
-        ld_jn(2, 1)
-        exit_phi(2, 0)
-        exit_phi(2, 1)
-        exit_phi(2, 2)
-        exit_phi(2, 3)
-        il_w(0, 1, S)
-        flip_force(0, 1)
-        ld_w(1, 1)
-        ld_force(2)
-        q_phi(2)
-        exit_force(0, 0)
-        flip_force(0, 2)
-        stt(1, 0)
-        exit_force(0, 1)
-        warm(8)
-        q_pose(1)
-        flip_force(1, 2)
-        ld_jn(1, 1)
-        q_wg(0)
-        q_w(0, 1)
-        flip_force(1, 0)
-        ld_wg(1)
-        il_jac(0, 0, V)
+        flip_phi(2, 2)
         exit_force(0, 2)
-        q_force(0, 0)
-        il_w(1, 1, S)
-        q_jac(0, 0)
-        il_jac(1, 0, V)
-        exit_force(1, 0)
-        exit_force(1, 2)
-        ja(2, 0, S)
-        mm1(2, 0)
-        flip_force(1, 1)
-        mm2(0, 0, -1)
-        mm2(0, 0, 0)
-        mm2(2, 0, -1)
-        q_w(1, 1)
-        mm1(0, 1)
         q_force(0, 1)
-        mm2(2, 0, 0)
-        mm2(1, 0, -1)
-        stt(2, 0)
-        ld_jn(0, 1)
-        mm2(1, 0, 0)
+        warm(12)
+        exit_force(0, 0)
+        q_phi(1)
+        stt(0, 0)
+        exit_phi(2, 3)
+        flip_phi(2, 0)
+        q_pose(0)
+        flip_phi(2, 1)
+        exit_phi(2, 2)
+        mm1(1, 0)
+        exit_phi(2, 0)
+        q_w(0, 1)
+        exit_phi(2, 1)
+        q_phi(2)
+        il_jac(0, 0, S)
+        stt(1, 0)
+        il_w(1, 1, S)
+        flip_force(1, 1)
+        ld_jn(1, 1)
+        warm(13)
+        il_wg(0, V)
         exit_force(1, 1)
-        mm2(3, 0, -1)
-        q_jac(1, 0)
-        mm2(3, 0, 0)
-        il_jac(2, 0, V)
-        mm2(2, 0, 1)
-        mm2(0, 0, 1)
+        flip_pose(1)
+        ld_jn(2, 0)
+        ld_wg(1)
+        ja(2, 0, S)
+        exit_pose(1)
+        mm1(2, 0)
+        q_w(1, 1)
+        flip_force(1, 2)
+        mm1(0, 1)
+        flip_force(1, 0)
+        q_wg(0)
+        q_force(0, 0)
+        mm2(2, 0, -1)
+        exit_force(1, 2)
+        mm2(0, 0, -1)
+        stt(2, 0)
+        q_jac(0, 0)
         q_force(0, 2)
-        ja(0, 1, S)
-        mm2(3, 0, 1)
+        mm2(0, 0, 0)
+        mm2(3, 0, -1)
+        mm2(1, 0, -1)
+        mm2(2, 0, 0)
+        il_jac(1, 0, V)
+        il_jac(2, 0, V)
+        q_jac(1, 0)
         q_jac(2, 0)
+        mm2(1, 0, 0)
+        ld_jn(0, 1)
+        exit_force(1, 0)
+        ja(0, 1, S)
+        mm2(3, 0, 0)
+        ja(2, 1, S)
+        mm2(0, 0, 1)
+        mm2(2, 0, 1)
         mm2(1, 0, 1)
         stt(0, 1)
+        q_pose(1)
         mm2(0, 0, 2)
-        il_wg(1, S)
-        q_force(1, 0)
         mm2(1, 0, 2)
         q_force(1, 1)
-        mm2(2, 0, 2)
-        mm1(2, 1)
-        mm2(3, 0, 2)
-        mm2(5, 0, -1)
-        mm2(5, 0, 0)
-        mm2(6, 0, -1)
-        mm2(4, 0, -1)
-        mm2(7, 0, -1)
-        mm2(4, 0, 0)
         store(0, 0, S)
+        mm2(3, 0, 1)
+        mm2(2, 0, 2)
         store(2, 0, S)
+        mm2(3, 0, 2)
+        mm1(2, 1)
+        q_force(1, 0)
+        mm2(5, 0, -1)
+        mm2(4, 0, -1)
+        il_wg(1, V)
+        store(3, 0, S)
+        mm2(4, 0, 0)
+        mm2(7, 0, -1)
+        mm2(6, 0, -1)
+        mm2(5, 0, 0)
+        mm2(4, 0, 1)
+        mm2(7, 0, 0)
         q_force(1, 2)
-        ja(2, 1, V)
+        mm2(5, 0, 1)
+        mm2(4, 0, 2)
+        mm2(6, 0, 0)
+        mm2(5, 0, 2)
+        mm2(6, 0, 1)
+        mm2(7, 0, 1)
         store(1, 0, S)
         q_wg(1)
-        mm2(5, 0, 1)
-        mm2(7, 0, 0)
-        mm2(7, 0, 1)
-        mm2(4, 0, 1)
-        store(3, 0, S)
-        mm2(4, 0, 2)
-        mm2(5, 0, 2)
         il_jac(0, 1, S)
-        mm2(6, 0, 0)
-        mm2(6, 0, 1)
-        mm2(6, 0, 2)
-        stt(2, 1)
         ja(1, 1, S)
         mm1(1, 1)
-        mm2(1, 1, -1)
-        stt(1, 1)
-        mm2(7, 0, 2)
-        store(6, 0, S)
-        store(5, 0, S)
-        mm2(7, 1, -1)
-        mm2(6, 1, -1)
-        q_jac(0, 1)
         mm2(3, 1, -1)
-        mm2(4, 1, -1)
-        mm2(5, 1, -1)
-        mm2(7, 1, 0)
-        mm2(2, 1, -1)
-        store(4, 0, S)
-        il_jac(1, 1, V)
-        mm2(1, 1, 0)
-        mm2(4, 1, 0)
         mm2(0, 1, -1)
+        mm2(6, 0, 2)
+        mm2(7, 1, -1)
+        mm2(7, 0, 2)
+        store(4, 0, S)
+        store(5, 0, S)
+        stt(2, 1)
+        stt(1, 1)
+        mm2(5, 1, -1)
+        mm2(1, 1, -1)
+        mm2(4, 1, -1)
+        q_jac(0, 1)
+        mm2(1, 1, 0)
         mm2(0, 1, 0)
-        store(7, 0, S)
-        mm2(6, 1, 0)
-        mm2(5, 1, 0)
-        q_jac(1, 1)
         il_jac(2, 1, S)
+        mm2(7, 1, 0)
+        mm2(6, 1, -1)
+        il_jac(1, 1, V)
+        mm2(3, 1, 0)
+        mm2(5, 1, 0)
+        store(7, 0, S)
+        mm2(4, 1, 0)
+        q_jac(1, 1)
         q_jac(2, 1)
-        mm2(6, 1, 1)
-        mm2(4, 1, 1)
+        mm2(6, 1, 0)
         mm2(1, 1, 1)
+        mm2(4, 1, 1)
         mm2(4, 1, 2)
         mm2(1, 1, 2)
-        mm2(0, 1, 1)
-        mm2(3, 1, 0)
-        store(4, 1, S)
-        mm2(0, 1, 2)
-        mm2(6, 1, 2)
-        mm2(5, 1, 1)
-        mm2(7, 1, 1)
-        mm2(5, 1, 2)
-        mm2(7, 1, 2)
-        store(1, 1, S)
+        store(6, 0, S)
+        store(4, 1, V)
         mm2(3, 1, 1)
-        store(0, 1, V)
+        mm2(5, 1, 1)
+        store(1, 1, S)
+        mm2(5, 1, 2)
+        mm2(7, 1, 1)
+        mm2(7, 1, 2)
+        mm2(6, 1, 1)
+        mm2(6, 1, 2)
+        mm2(0, 1, 1)
+        store(5, 1, V)
         mm2(3, 1, 2)
-        store(6, 1, S)
-        store(5, 1, S)
+        store(7, 1, S)
+        mm2(0, 1, 2)
+        mm2(2, 1, -1)
+        store(6, 1, V)
+        store(3, 1, V)
+        store(0, 1, V)
         mm2(2, 1, 0)
         mm2(2, 1, 1)
         mm2(2, 1, 2)
-        store(7, 1, V)
-        store(3, 1, S)
         store(2, 1, S)

from contextlib import ExitStack

import concourse.mybir as mybir
from concourse.masks import make_identity

C, K, D, B, L = 1536, 1024, 1024, 1024, 512
FLOPS = 2 * C * K * D + 2 * B * C * D + 2 * B * L * D

F32 = mybir.dt.float32
BF16 = mybir.dt.bfloat16
U32 = mybir.dt.uint32
U8 = mybir.dt.uint8
FP8 = mybir.dt.float8_e4m3fn
FP8X4 = mybir.dt.float8_e4m3fn_x4
MULT = mybir.AluOpType.mult
ADD = mybir.AluOpType.add
COPY = mybir.ActivationFunctionType.Copy


def tile_contact_jacobian_torque_s7_kernel(tc, phi_bytes, phi_scale, w, j_nom, act, force, pose, wg, out):
    nc = tc.nc
    V = nc.vector
    S = nc.scalar
    with ExitStack() as ctx:
        keep = ctx.enter_context(tc.tile_pool(name="keep", bufs=1))
        work = ctx.enter_context(tc.tile_pool(name="work", bufs=1))
        psum = ctx.enter_context(tc.psum_pool(name="psum", bufs=8))
        ctx.enter_context(tc.manual_schedule())

        zeros = keep.tile([128, 512], BF16, name="zeros", align_bytes=64)
        nc.gpsimd.memset(zeros[:], 0.0)
        ident = keep.tile([128, 128], F32, name="ident")
        make_identity(nc, ident[:])
        scale = keep.tile([128, K], F32, name="scale")
        act16 = keep.tile([128, 3, 4], BF16, name="act16")
        nc.scalar.dma_start(out=act16[:], in_=act.rearrange("(g p t) -> p g t", p=128, t=4))
        nc.scalar.dma_start(out=scale[:], in_=phi_scale.rearrange("o k -> (o k)").partition_broadcast(128))
        act32 = keep.tile([128, 3, 4], F32, name="act32")
        nc.gpsimd.tensor_copy(out=act32[:], in_=act16[:])

        held = {}
        w_v = w.rearrange("(g p t) n -> g p t n", p=128, t=4)
        phi_v = phi_bytes.rearrange("(g m t) k -> g m t k", m=128, t=4)
        jn_v = j_nom.rearrange("(g m t) d -> g m t d", m=128, t=4)
        force_v = force.rearrange("(p j) c -> p j c", j=8)
        pose_v = pose.rearrange("(p j) l -> p j l", j=8)
        wg_v = wg.rearrange("(p t) n -> p t n", t=4)
        out_v = out.rearrange("(p j) d -> j p d", j=8)

        raw = {}

        def raw_tile(key):
            t = work.tile([128, 4, 512], BF16, name="raw", tag="raw", bufs=5, align_bytes=64)
            raw[key] = t
            return t

        phi_raw = {}
        jn_raw = {}
        f_raw = [work.tile([128, 2, C], BF16, name="f_raw%d" % i, tag="f_raw", bufs=4, align_bytes=64) for i in range(4)]

        def ld_w(g, h):
            x = raw_tile(("w", g, h))
            nc.sync.dma_start(out=x[:], in_=w_v[g][:, :, 512 * h:512 * (h + 1)])

        def ld_phi(G):
            phi_raw[G] = work.tile([128, 4, K], U8, name="phi_raw", tag="phi_raw", bufs=3, align_bytes=64)
            nc.sync.dma_start(out=phi_raw[G][:], in_=phi_v[G])

        def ld_jn(G, h):
            x = work.tile([128, 4, 512], BF16, name="jn_raw", tag="jn_raw", bufs=6, align_bytes=64)
            jn_raw[G, h] = x
            nc.sync.dma_start(out=x[:], in_=jn_v[G][:, :, 512 * h:512 * (h + 1)])

        def ld_force(i):
            nc.sync.dma_start(out=f_raw[i][:], in_=force_v[:, 2 * i:2 * i + 2, :])

        def ld_wg(h):
            x = raw_tile(("wg", h))
            nc.sync.dma_start(out=x[:], in_=wg_v[:, :, 512 * h:512 * (h + 1)])

        def ld_pose(jh):
            x = raw_tile(("p", jh))
            nc.sync.dma_start(out=x[:], in_=pose_v[:, 4 * jh:4 * jh + 4, :])


        phi_c = keep.tile([128, 3, 2, 512], U32, name="phi_c", align_bytes=64)
        phi_s = keep.tile([128, 3, 2, 512], U8, name="phi_s", align_bytes=64)
        w_c = keep.tile([128, 2, D], U32, name="w_c", align_bytes=64)
        w_s = keep.tile([128, 2, D], U8, name="w_s", align_bytes=64)
        jac_c = keep.tile([128, 3, D], U32, name="jac_c", align_bytes=64)
        jac_s = keep.tile([128, 3, D], U8, name="jac_s", align_bytes=64)
        f_c = keep.tile([128, 3, B], U32, name="f_c", align_bytes=64)
        f_s = keep.tile([128, 3, B], U8, name="f_s", align_bytes=64)
        p_c = keep.tile([128, B], U32, name="p_c", align_bytes=64)
        p_s = keep.tile([128, B], U8, name="p_s", align_bytes=64)
        wg_c = keep.tile([128, D], U32, name="wg_c", align_bytes=64)
        wg_s = keep.tile([128, D], U8, name="wg_s", align_bytes=64)

        def grp_tile(key):
            t = work.tile([128, 512, 4], BF16, name="grp", tag="grp", bufs=7, align_bytes=64)
            held[key] = t
            return t

        def bank(key, ring, dtype=F32):
            t = psum.tile([128, 2048 // (4 if dtype == F32 else 2)], dtype, name="bank_" + ring, tag="bank_" + ring, bufs=4)
            held[key] = t
            return t

        def warm(i):
            x = bank(("warm", i), "b")
            for k in range(2):
                nc.tensor.matmul(x[:], zeros[:, 0:128], zeros[:], start=True, stop=True)

        def copy_on(eng, dst, src):
            if eng is V:
                nc.vector.tensor_copy(out=dst, in_=src)
            else:
                nc.scalar.copy(out=dst, in_=src)

        def interleave(eng, key, src):
            t = grp_tile(key)
            copy_on(eng, t[:].rearrange("p (c i) t -> p c t i", i=4), src.rearrange("p t (c i) -> p c t i", i=4))

        def quantize(key, codes, scales):
            nc.vector.quantize_mx(out=codes.bitcast(FP8X4), scales=scales, in_=held[key][:].rearrange("p n t -> p (n t)"))

        def il_w(g, h, eng):
            interleave(eng, ("w", g, h), raw["w", g, h][:])

        def q_w(g, h):
            cols = slice(512 * h, 512 * (h + 1))
            quantize(("w", g, h), w_c[:, g, cols], w_s[:, g, cols])

        def il_wg(h, eng):
            interleave(eng, ("wg", h), raw["wg", h][:])

        def q_wg(h):
            cols = slice(512 * h, 512 * (h + 1))
            quantize(("wg", h), wg_c[:, cols], wg_s[:, cols])

        def prod(G, t):
            x = work.tile([128, K], BF16, name="ph", tag="ph", bufs=4, align_bytes=64)
            held["ph", G, t] = x
            nc.vector.tensor_tensor(out=x[:], in0=phi_raw[G][:, t, :].bitcast(FP8), in1=scale[:], op=MULT)

        def flip_phi(G, t):
            words = held["ph", G, t][:].bitcast(F32)
            x = bank(("flip", G, t), "a")
            x4 = x[:].rearrange("p (g u m) -> p g u m", g=2, u=2)
            for g in range(2):
                for u in range(2):
                    nc.tensor.transpose(x4[:, g, u, :], words[:, 256 * g + u:256 * (g + 1):2], ident[:])

        def exit_phi(G, t):
            if ("gphi", G) not in held:
                held["gphi", G] = work.tile([128, 2, 512, 4], BF16, name="gphi", tag="gphi", bufs=2, align_bytes=64)
            x4 = held["flip", G, t][:].rearrange("p (g u m) -> p g u m", g=2, u=2)
            dst = held["gphi", G][:].rearrange("p g n t -> p (g n t)").bitcast(F32).rearrange("p (g n u) -> p g n u", g=2, u=2)
            nc.scalar.copy(out=dst[:, :, 128 * t:128 * (t + 1), :], in_=x4.rearrange("p g u m -> p g m u"))

        def q_phi(G):
            nc.vector.quantize_mx(
                out=phi_c[:, G, :, :].rearrange("p g n -> p (g n)").bitcast(FP8X4),
                scales=phi_s[:, G, :, :].rearrange("p g n -> p (g n)"),
                in_=held["gphi", G][:].rearrange("p g n t -> p (g n t)"),
            )

        def mm1(G, h):
            cols = slice(512 * h, 512 * (h + 1))
            for t in range(4):
                x = bank(("corr", G, h, t), "b")
                for g in range(2):
                    nc.tensor.matmul_mx(
                        out=x[:],
                        lhsT=phi_c[:, G, g, 128 * t:128 * (t + 1)].bitcast(FP8X4),
                        lhsT_scale=phi_s[:, G, g, 128 * t:128 * (t + 1)],
                        rhs=w_c[:, g, cols].bitcast(FP8X4),
                        rhs_scale=w_s[:, g, cols],
                        start=(g == 0), stop=(g == 1),
                    )

        def ja(G, h, eng):
            for t in range(4):
                x = work.tile([128, 512], F32, name="ja", tag="ja", bufs=8, align_bytes=64)
                held["ja", G, h, t] = x
                src = jn_raw[G, h][:, t, :]
                if eng is V:
                    nc.vector.tensor_scalar(out=x[:], in0=src, scalar1=act32[:, G, t:t + 1], scalar2=None, op0=MULT)
                else:
                    nc.scalar.activation(out=x[:], in_=src, func=COPY, scale=act32[:, G, t:t + 1])

        def stt(G, h):
            x = work.tile([128, 4, 512], BF16, name="jac", tag="jac", bufs=2, align_bytes=64)
            held["jac", G, h] = x
            for t in range(4):
                nc.vector.scalar_tensor_tensor(
                    out=x[:, t, :], in0=held["corr", G, h, t][:], scalar=act32[:, G, t:t + 1],
                    in1=held["ja", G, h, t][:], op0=MULT, op1=ADD)

        def il_jac(G, h, eng):
            interleave(eng, ("gjac", G, h), held["jac", G, h][:])

        def q_jac(G, h):
            cols = slice(512 * h, 512 * (h + 1))
            quantize(("gjac", G, h), jac_c[:, G, cols], jac_s[:, G, cols])

        def flip_rows(key, half, pr, words, first):
            x = bank(key + (pr,), "a")
            x4 = x[:].rearrange("p (j u m) -> p j u m", j=2, u=2)
            for j in range(2):
                for u in range(2):
                    nc.tensor.transpose(x4[:, j, u, :], words[:, first + j, half + u:half + 256:2], ident[:])

        def exit_rows(key, pr):
            if pr == 0:
                grp_tile(key)
            x4 = held[key + (pr,)][:].rearrange("p (j u m) -> p j u m", j=2, u=2)
            dst = held[key][:].rearrange("p n t -> p (n t)").bitcast(F32).rearrange("p (j m u) -> p j m u", j=4, u=2)
            nc.scalar.copy(out=dst[:, 2 * pr:2 * pr + 2, :, :], in_=x4.rearrange("p j u m -> p j m u"))

        def flip_force(jh, G):
            for pr in range(2):
                flip_rows(("f", jh, G), 256 * G, pr, f_raw[2 * jh + pr][:].bitcast(F32), 0)

        def exit_force(jh, G):
            for pr in range(2):
                exit_rows(("f", jh, G), pr)

        def exit_pose(jh):
            for pr in range(2):
                exit_rows(("p", jh), pr)

        def q_force(jh, G):
            cols = slice(512 * jh, 512 * (jh + 1))
            quantize(("f", jh, G), f_c[:, G, cols], f_s[:, G, cols])

        def flip_pose(jh):
            for pr in range(2):
                flip_rows(("p", jh), 0, pr, raw["p", jh][:].bitcast(F32), 2 * pr)

        def q_pose(jh):
            cols = slice(512 * jh, 512 * (jh + 1))
            quantize(("p", jh), p_c[:, cols], p_s[:, cols])

        def mm2_pass(j, h, lc, ls, rc, rs, start, stop):
            rows = slice(128 * j, 128 * (j + 1))
            cols = slice(512 * h, 512 * (h + 1))
            nc.tensor.matmul_mx(
                out=held["o", j, h][:], lhsT=lc[:, rows].bitcast(FP8X4), lhsT_scale=ls[:, rows],
                rhs=rc[:, cols].bitcast(FP8X4), rhs_scale=rs[:, cols], start=start, stop=stop)

        def mm2(j, h, G):
            if G < 0:
                bank(("o", j, h), "b" if h == 1 and j % 2 == 1 else "a")
                mm2_pass(j, h, p_c, p_s, wg_c, wg_s, True, False)
            else:
                mm2_pass(j, h, f_c[:, G, :], f_s[:, G, :], jac_c[:, G, :], jac_s[:, G, :], False, G == 2)

        def store(j, h, eng):
            x = work.tile([128, 512], F32, name="o_sb", tag="o_sb", bufs=5, align_bytes=64)
            copy_on(eng, x[:], held["o", j, h][:])
            nc.sync.dma_start(out=out_v[j][:, 512 * h:512 * (h + 1)], in_=x[:])


        warm(0)
        warm(1)
        ld_w(1, 0)
        ld_pose(0)
        warm(2)
        warm(3)
        ld_phi(1)
        il_w(1, 0, V)
        flip_pose(0)
        q_w(1, 0)
        prod(1, 0)
        prod(1, 1)
        warm(4)
        flip_phi(1, 0)
        ld_w(0, 1)
        prod(1, 2)
        ld_phi(0)
        exit_pose(0)
        ld_w(0, 0)
        prod(1, 3)
        prod(0, 0)
        ld_force(0)
        ld_force(1)
        flip_phi(1, 1)
        warm(5)
        il_w(0, 1, S)
        flip_phi(1, 2)
        exit_phi(1, 0)
        exit_phi(1, 1)
        ld_phi(2)
        ld_jn(0, 0)
        prod(0, 1)
        exit_phi(1, 2)
        ld_w(1, 1)
        prod(0, 2)
        warm(6)
        flip_phi(1, 3)
        warm(7)
        ld_jn(1, 0)
        flip_phi(0, 0)
        ld_force(2)
        il_w(0, 0, S)
        warm(8)
        exit_phi(0, 0)
        ld_pose(1)
        flip_phi(0, 1)
        q_w(0, 0)
        prod(0, 3)
        exit_phi(1, 3)
        flip_phi(0, 2)
        warm(9)
        prod(2, 0)
        flip_force(0, 1)
        exit_phi(0, 2)
        prod(2, 1)
        flip_phi(0, 3)
        warm(10)
        exit_phi(0, 1)
        exit_force(0, 1)
        flip_force(0, 2)
        exit_phi(0, 3)
        ld_wg(0)
        q_phi(0)
        warm(11)
        prod(2, 2)
        prod(2, 3)
        flip_force(0, 0)
        ja(0, 0, S)
        ld_jn(2, 1)
        ld_force(3)
        ja(1, 0, S)
        mm1(0, 0)
        flip_phi(2, 3)
        flip_phi(2, 2)
        exit_force(0, 2)
        q_force(0, 1)
        warm(12)
        exit_force(0, 0)
        q_phi(1)
        stt(0, 0)
        exit_phi(2, 3)
        flip_phi(2, 0)
        q_pose(0)
        flip_phi(2, 1)
        exit_phi(2, 2)
        mm1(1, 0)
        exit_phi(2, 0)
        q_w(0, 1)
        exit_phi(2, 1)
        q_phi(2)
        il_jac(0, 0, S)
        stt(1, 0)
        il_w(1, 1, S)
        flip_force(1, 1)
        ld_jn(1, 1)
        warm(13)
        il_wg(0, V)
        exit_force(1, 1)
        flip_pose(1)
        ld_jn(2, 0)
        ld_wg(1)
        ja(2, 0, S)
        exit_pose(1)
        mm1(2, 0)
        q_w(1, 1)
        flip_force(1, 2)
        mm1(0, 1)
        flip_force(1, 0)
        q_wg(0)
        q_force(0, 0)
        mm2(2, 0, -1)
        exit_force(1, 2)
        mm2(0, 0, -1)
        stt(2, 0)
        q_jac(0, 0)
        q_force(0, 2)
        mm2(0, 0, 0)
        mm2(3, 0, -1)
        mm2(1, 0, -1)
        mm2(2, 0, 0)
        il_jac(1, 0, V)
        il_jac(2, 0, V)
        q_jac(1, 0)
        q_jac(2, 0)
        mm2(1, 0, 0)
        ld_jn(0, 1)
        exit_force(1, 0)
        ja(0, 1, S)
        mm2(3, 0, 0)
        ja(2, 1, S)
        mm2(0, 0, 1)
        mm2(2, 0, 1)
        mm2(1, 0, 1)
        stt(0, 1)
        q_pose(1)
        mm2(0, 0, 2)
        mm2(1, 0, 2)
        q_force(1, 1)
        store(0, 0, S)
        mm2(3, 0, 1)
        mm2(2, 0, 2)
        store(2, 0, S)
        mm2(3, 0, 2)
        mm1(2, 1)
        q_force(1, 0)
        mm2(5, 0, -1)
        mm2(4, 0, -1)
        il_wg(1, V)
        store(3, 0, S)
        mm2(4, 0, 0)
        mm2(7, 0, -1)
        mm2(6, 0, -1)
        mm2(5, 0, 0)
        mm2(4, 0, 1)
        mm2(7, 0, 0)
        q_force(1, 2)
        mm2(5, 0, 1)
        mm2(4, 0, 2)
        mm2(6, 0, 0)
        mm2(5, 0, 2)
        mm2(6, 0, 1)
        mm2(7, 0, 1)
        store(1, 0, S)
        q_wg(1)
        il_jac(0, 1, S)
        ja(1, 1, S)
        mm1(1, 1)
        mm2(3, 1, -1)
        mm2(0, 1, -1)
        mm2(6, 0, 2)
        mm2(7, 1, -1)
        mm2(7, 0, 2)
        store(4, 0, S)
        store(5, 0, S)
        stt(2, 1)
        stt(1, 1)
        mm2(5, 1, -1)
        mm2(1, 1, -1)
        mm2(4, 1, -1)
        q_jac(0, 1)
        mm2(1, 1, 0)
        mm2(0, 1, 0)
        il_jac(2, 1, S)
        mm2(7, 1, 0)
        mm2(6, 1, -1)
        il_jac(1, 1, V)
        mm2(3, 1, 0)
        mm2(5, 1, 0)
        store(7, 0, S)
        mm2(4, 1, 0)
        q_jac(1, 1)
        q_jac(2, 1)
        mm2(6, 1, 0)
        mm2(1, 1, 1)
        mm2(4, 1, 1)
        mm2(4, 1, 2)
        mm2(1, 1, 2)
        store(6, 0, S)
        store(4, 1, V)
        mm2(3, 1, 1)
        mm2(5, 1, 1)
        store(1, 1, S)
        mm2(5, 1, 2)
        mm2(7, 1, 1)
        mm2(7, 1, 2)
        mm2(6, 1, 1)
        mm2(6, 1, 2)
        mm2(0, 1, 1)
        store(5, 1, V)
        mm2(3, 1, 2)
        store(7, 1, S)
        mm2(0, 1, 2)
        mm2(2, 1, -1)
        store(6, 1, V)
        store(3, 1, V)
        store(0, 1, V)
        mm2(2, 1, 0)
        mm2(2, 1, 1)
        mm2(2, 1, 2)
        store(2, 1, S)
